import numpy as np
import ml_dtypes


def mxq(x, axis, fmt="e4m3"):
    dtype, down = {"e4m3": (ml_dtypes.float8_e4m3fn, 7), "e5m2": (ml_dtypes.float8_e5m2, 14)}[fmt]
    v = np.moveaxis(np.asarray(x, np.float32).astype(ml_dtypes.bfloat16).astype(np.float64), axis, -1)
    blocks = v.reshape(v.shape[:-1] + (-1, 32))
    amax = np.abs(blocks).max(-1, keepdims=True)
    byte = np.maximum(np.where(amax > 0, np.frexp(amax)[1] - 1 + 127, 0) - down, 1)
    scale = np.exp2(byte - 127.0)
    codes = (blocks / scale).astype(np.float32).astype(dtype).astype(np.float64)
    return np.moveaxis((codes * scale).reshape(v.shape), -1, axis)


WIDE = False


def mx_kscale(k):
    if not WIDE:
        return np.ones(k)
    levels = np.array([10, -10, 5, -5, 0])
    if k % 512:
        return np.exp2(np.random.permutation(np.resize(levels, k // 32))).repeat(32)
    a = np.empty((k // 512, 16))
    for p in range(k // 512):
        a[p, :8] = np.random.permutation(np.resize(levels, 8))
        for g in range(8):
            far = levels[np.abs(levels - a[p, g]) >= 10]
            a[p, g + 8] = far[np.random.randint(len(far))]
    return np.exp2(a.ravel()).repeat(32)


def f64(x):
    return np.asarray(x).astype(np.float64)


def striped(idx):
    return np.tile(idx.reshape(-1, 16).T, (8, 1)).astype(np.uint16)


def unstriped(offs):
    return offs[:16].T.reshape(-1).astype(np.int64)


E2M1 = np.array([0.0, 0.5, 1.0, 1.5, 2.0, 3.0, 4.0, 6.0, -0.0, -0.5, -1.0, -1.5, -2.0, -3.0, -4.0, -6.0])


def pack_weight(w, fmt):
    k, n = w.shape
    w = f64(np.asarray(w, np.float32).astype(ml_dtypes.bfloat16)).reshape(k // 32, 32, n)
    amax = np.abs(w).max(1)
    if fmt == "e4m3":
        byte = np.frexp(amax)[1] - 1 + 127 - 7
    else:
        mant, ex = np.frexp(amax / 6.0)
        byte = np.where(mant > 0.5, ex, ex - 1) + 127
    byte = np.clip(np.where(amax > 0, byte, 1), 1, 254)
    scaled = (w * np.exp2(127.0 - byte)[:, None, :]).reshape(k, n).astype(np.float32)
    by_word = np.ascontiguousarray(scaled.reshape(k // 512, 128, 4, n).transpose(0, 1, 3, 2))
    if fmt == "e4m3":
        words = by_word.astype(ml_dtypes.float8_e4m3fn).view(np.uint8)
    else:
        c = by_word.astype(ml_dtypes.float4_e2m1fn).view(np.uint8) & 0xF
        words = (c[..., 0::2] | (c[..., 1::2] << 4)).reshape(k // 512, 128, 2 * n)
    return np.ascontiguousarray(words), np.ascontiguousarray(byte.astype(np.uint8).reshape(k // 512, 16, n))


def unpack_weight(words, scales, fmt):
    g, _, n = scales.shape
    words = np.ascontiguousarray(words).reshape(g, 128, n, -1)
    if fmt == "e4m3":
        vals = words.view(ml_dtypes.float8_e4m3fn).astype(np.float64)
    else:
        nib = np.empty((g, 128, n, 4), np.uint8)
        nib[..., 0::2] = words & 0xF
        nib[..., 1::2] = words >> 4
        vals = E2M1[nib]
    vals = vals * np.repeat(np.exp2(scales.astype(np.float64) - 127.0), 8, axis=1)[..., None]
    return vals.transpose(0, 1, 3, 2).reshape(g * 512, n)


def gelu(v):
    return 0.5 * v * (1.0 + np.tanh(np.sqrt(2.0 / np.pi) * (v + 0.044715 * v**3)))


K, K2, H, N, T, TB, S, P = 1024, 512, 1024, 384, 4096, 2048, 1024, 512

def setup_inputs():
    n = np.random.standard_normal
    s = mx_kscale(K)[:, None]
    s2 = mx_kscale(K2)[:, None]
    u = mx_kscale(H)[:, None]
    d = {}
    d["tab_words"], d["tab_scales"] = pack_weight(n((K, T)) * s, "e4m3")
    d["offs"] = striped(np.random.permutation(T)[:S])
    d["tab2_words"], d["tab2_scales"] = pack_weight(n((K2, TB)) * s2, "e4m3")
    d["offs2"] = striped(np.random.permutation(TB)[:P])
    d["pos1"] = striped(np.random.permutation(S)[:P])
    d["wa"] = (n((K, H)) / s * 1.5 / K ** 0.5).astype(np.float32)
    d["wb_words"], d["wb_scales"] = pack_weight(n((K2, H)) / s2 * 1.5 / K2 ** 0.5, "e2m1")
    d["wgs"] = np.exp(0.3 * n((128, P))).astype(np.float32)
    d["gz"] = (np.exp(0.3 * n(H)) * u[:, 0]).astype(np.float32)
    d["w2"] = (n((H, H)) / u * 1.2 / H ** 0.5).astype(np.float32)
    d["gt"] = (np.exp(0.3 * n(H)) * u[:, 0]).astype(np.float32)
    d["w3_words"], d["w3_scales"] = pack_weight(n((H, N)) / u / H ** 0.5, "e4m3")
    return d

def reference(tab_words, tab_scales, offs, tab2_words, tab2_scales, offs2, pos1, wa, wb_words, wb_scales, wgs, gz, w2, gt, w3_words, w3_scales):
    v = unpack_weight(tab_words, tab_scales, "e4m3")[:, unstriped(offs)]
    v2 = unpack_weight(tab2_words, tab2_scales, "e4m3")[:, unstriped(offs2)]
    pa = mxq(f64(wa), 0, "e4m3").T @ v
    a = pa / (1.0 + np.exp(-pa))
    q = unpack_weight(wb_words, wb_scales, "e2m1").T @ v2
    b = 1.0 / (1.0 + np.square(q))
    placed = np.zeros((H, S))
    placed[:, unstriped(pos1)] = np.tile(f64(wgs), (H // 128, 1)) * b
    z = f64(gz)[:, None] * (a + placed)
    t = np.tanh(mxq(f64(w2), 0, "e4m3").T @ mxq(z, 0, "e4m3"))
    y = z + f64(gt)[:, None] * t
    out = unpack_weight(w3_words, w3_scales, "e4m3").T @ mxq(y, 0, "e4m3")
    return out

@@ -1,0 +1,324 @@
+from contextlib import ExitStack
+
+import concourse.mybir as mybir
+
+F32 = mybir.dt.float32
+BF16 = mybir.dt.bfloat16
+I32 = mybir.dt.int32
+U32 = mybir.dt.uint32
+U16 = mybir.dt.uint16
+U8 = mybir.dt.uint8
+FP8X4 = mybir.dt.float8_e4m3fn_x4
+FP4X4 = mybir.dt.float4_e2m1fn_x4
+ACT = mybir.ActivationFunctionType
+MULT = mybir.AluOpType.mult
+ADD = mybir.AluOpType.add
+
+FLOPS = 5637144576
+
+P = 128
+PACK = 4
+KP = P * PACK
+T, TB, S, NP, H, N = 4096, 2048, 1024, 512, 1024, 384
+BANK = 512
+CHUNKS = ((0, 512), (512, 512))
+Y_WEAVE = (("vector","scalar"),("scalar","vector"))
+Z_WEAVE = ("vector","scalar")
+
+
+def tile_list_pitch_delivery_scores_kernel(
+    tc, tab_words, tab_scales, offs, tab2_words, tab2_scales, offs2, pos1, wa, wb_words, wb_scales,
+    wgs, gz, w2, gt, w3_words, w3_scales, out,
+):
+    nc = tc.nc
+    with ExitStack() as ctx:
+        keep = ctx.enter_context(tc.tile_pool(name="keep", bufs=1))
+        ring = ctx.enter_context(tc.tile_pool(name="ring", bufs=1))
+        psum = ctx.enter_context(tc.psum_pool(name="psum", bufs=8))
+
+        def held(name, shape, dtype, tag=None):
+            return keep.tile(shape, dtype, name=name, tag=tag or name, align_bytes=64)
+
+        def raw_tile(name):
+            return ring.tile([P, PACK, KP], F32, name=name, tag="raw", bufs=4, align_bytes=64)
+
+        def grouped_tile(name, cols):
+            return ring.tile([P, cols * PACK], BF16, name=name, tag="grouped", bufs=5, align_bytes=64)
+
+        def row_tile(name, cols):
+            return ring.tile([P, cols], F32, name=name, tag="row", bufs=8, align_bytes=64)
+
+        def bank_tile(name, cols):
+            return psum.tile([P, cols], F32, name=name, tag="bank")
+
+        offs_t = held("offs_t", [P, S // 16], U16)
+        offs2_t = held("offs2_t", [P, NP // 16], U16)
+        pos_t = held("pos_t", [P, NP // 16], U16)
+
+        tab2_w = held("tab2_w", [P, TB], I32)
+        tab2_s = held("tab2_s", [P, TB], U8)
+        wb_w = held("wb_w", [P, 2 * H], U8)
+        wb_s = held("wb_s", [P, H], U8)
+        tab_w = [held(f"tab_w{g}", [P, T], I32, tag=f"wide{g}") for g in range(2)]
+        tab_s = held("tab_s", [P, T], U8)
+        w3_w = held("w3_w", [P, 2, N], I32)
+        w3_s = held("w3_s", [P, 2 * N], U8)
+        wgs_t = held("wgs_t", [P, PACK * NP], F32)
+        gz_t = held("gz_t", [P, 2, PACK], F32)
+        gt_t = held("gt_t", [P, 2, PACK], F32)
+        one = held("one", [P, 1], F32)
+        warm = held("warm", [P, 1], F32)
+        placed = [held(f"placed{t}", [P, S], F32) for t in range(PACK + 1)]
+
+        nc.gpsimd.memset(tab2_s[:].bitcast(I32), 0)
+        nc.vector.memset(wb_s[:].bitcast(I32), 0)
+        nc.vector.memset(one[:], 1.0)
+        nc.vector.memset(tab_s[:].bitcast(I32), 0)
+        nc.vector.memset(w3_s[:].bitcast(I32), 0)
+        for page in placed:
+            nc.vector.memset(page[:], 0.0)
+        nc.scalar.activation(out=warm[:], in_=one[:], func=ACT.Abs_reciprocal_sqrt, bias=one[:])
+
+        nc.sync.dma_start(offs2_t[:], offs2)
+        nc.sync.dma_start(pos_t[:], pos1)
+        nc.sync.dma_start(gz_t[:], gz.rearrange("(a p t) -> p a t", a=2, t=PACK))
+        nc.sync.dma_start(offs_t[:], offs)
+        nc.sync.dma_start(gt_t[:], gt.rearrange("(a p t) -> p a t", a=2, t=PACK))
+        nc.sync.dma_start(wb_w[:].bitcast(I32), wb_words[0].bitcast(I32))
+        nc.sync.dma_start(tab2_w[:], tab2_words[0].rearrange("p t i -> p (t i)").bitcast(I32))
+        for q in range(4):
+            nc.sync.dma_start(wb_s[32 * q : 32 * q + 4, :].bitcast(I32), wb_scales[0, 4 * q : 4 * q + 4, :].bitcast(I32))
+        for q in range(4):
+            queue = nc.sync if q < 2 else nc.gpsimd
+            queue.dma_start(tab2_s[32 * q : 32 * q + 4, :].bitcast(I32), tab2_scales[0, 4 * q : 4 * q + 4, :].bitcast(I32))
+        for q in range(4):
+            nc.sync.dma_start(wgs_t[32 * q : 32 * q + 32, :], wgs.rearrange("(p t) j -> p (t j)", t=PACK))
+
+        def load_weight(w, name, g, h):
+            raw = raw_tile(f"{name}_raw{g}{h}")
+            nc.sync.dma_start(raw[:], w[KP * g : KP * (g + 1), KP * h : KP * (h + 1)].rearrange("(p i) c -> p i c", i=PACK))
+            return raw
+
+        for q in range(4):
+            nc.sync.dma_start(tab_s[32 * q : 32 * q + 8, :].bitcast(I32), tab_scales[:, 4 * q : 4 * q + 4, :].bitcast(I32))
+        wa_raw = {(g, 0): load_weight(wa, "wa", g, 0) for g in range(2)}
+        for g in range(2):
+            nc.sync.dma_start(tab_w[g][:], tab_words[g].rearrange("p t i -> p (t i)").bitcast(I32))
+        for g in range(2):
+            wa_raw[g, 1] = load_weight(wa, "wa", g, 1)
+        quarters = [(g, h) for h in range(2) for g in range(2)]
+        w2_raw = {gh: load_weight(w2, "w2", *gh) for gh in quarters}
+        for q in range(4):
+            nc.sync.dma_start(
+                w3_s[32 * q : 32 * q + 4, :].bitcast(I32).rearrange("r (g n) -> r g n", g=2),
+                w3_scales[:, 4 * q : 4 * q + 4, :].bitcast(I32).rearrange("g r n -> r g n"),
+            )
+        nc.sync.dma_start(w3_w[:], w3_words.rearrange("g p n i -> p g (n i)").bitcast(I32))
+
+        def quantise(name, grouped, cols):
+            codes = held(f"{name}_c", [P, cols], U32)
+            scales = held(f"{name}_s", [P, cols], U8)
+            nc.vector.quantize_mx(out=codes[:].bitcast(FP8X4), scales=scales[:], in_=grouped[:])
+            return codes, scales
+
+        def quantise_weight(name, raw):
+            grouped = grouped_tile(f"{name}_grouped", KP)
+            nc.scalar.copy(
+                out=grouped[:].rearrange("p (t m i) -> p m i t", t=PACK, i=PACK),
+                in_=raw[:].rearrange("p i (m t) -> p m i t", t=PACK),
+            )
+            return quantise(name, grouped, KP)
+
+        def product(acc, stationary, col0, moving):
+            cols = slice(col0, col0 + P)
+            for g in range(2):
+                nc.tensor.matmul_mx(
+                    out=acc,
+                    lhsT=stationary[g][0][:, cols].bitcast(FP8X4),
+                    lhsT_scale=stationary[g][1][:, cols],
+                    rhs=moving[g][0].bitcast(FP8X4),
+                    rhs_scale=moving[g][1],
+                    start=(g == 0),
+                    stop=(g == 1),
+                )
+
+        wbd_w = held("wbd_w", [P, 2 * H], U8)
+        wbd_s = held("wbd_s", [P, H], U8)
+        v2_w = held("v2_w", [P, NP], U32)
+        v2_s = held("v2_s", [P, NP], U8)
+        nc.vector.tensor_copy(
+            out=wbd_w[:].bitcast(U16).rearrange("p (a t m) -> p a t m", a=2, t=PACK),
+            in_=wb_w[:].bitcast(U16).rearrange("p (a m t) -> p a t m", a=2, t=PACK),
+        )
+        def deal_scales(a):
+            cols = slice(KP * a, KP * (a + 1))
+            nc.vector.tensor_copy(
+                out=wbd_s[:, cols].rearrange("p (t m) -> p t m", t=PACK), in_=wb_s[:, cols].rearrange("p (m t) -> p t m", t=PACK)
+            )
+
+        deal_scales(0)
+        nc.vector.tensor_copy(out=v2_s[:], in_=tab2_s[:].indirect(offs2_t[:]))
+        nc.vector.tensor_copy(out=v2_w[:], in_=tab2_w[:].bitcast(U32).indirect(offs2_t[:]))
+        deal_scales(1)
+
+        b = {}
+        gain = {}
+
+        def throws(a, t):
+            c0 = KP * a + P * t
+            bank = bank_tile(f"q{a}{t}", NP)
+            nc.tensor.matmul_mx(
+                out=bank[:],
+                lhsT=wbd_w[:, 2 * c0 : 2 * (c0 + P)].bitcast(FP4X4),
+                lhsT_scale=wbd_s[:, c0 : c0 + P],
+                rhs=v2_w[:].bitcast(FP8X4),
+                rhs_scale=v2_s[:],
+                start=True,
+                stop=True,
+            )
+            b[a, t] = row_tile(f"b{a}{t}", NP)
+            parts = [slice(0, NP // 2), slice(NP // 2, NP)] if (a, t) == (0, 0) else [slice(0, NP)]
+            for cols in parts:
+                nc.scalar.activation(out=b[a, t][:, cols], in_=bank[:, cols], func=ACT.Square)
+            for cols in parts:
+                nc.scalar.activation(out=b[a, t][:, cols], in_=b[a, t][:, cols], func=ACT.Abs_reciprocal_sqrt, bias=one[:])
+            for cols in parts:
+                nc.scalar.activation(out=b[a, t][:, cols], in_=b[a, t][:, cols], func=ACT.Square)
+            gain[a, t] = held(f"gain{a}{t}", [P, NP], F32)
+            nc.vector.tensor_scalar(
+                out=gain[a, t][:], in0=wgs_t[:, NP * t : NP * (t + 1)], scalar1=gz_t[:, a, t : t + 1], scalar2=None, op0=MULT
+            )
+
+        def page_of(a, t):
+            return placed[t if a == 0 else (4, 1, 3, 3)[t]]
+
+        def place(a, t):
+            nc.vector.tensor_tensor(out=page_of(a, t)[:].indirect(pos_t[:]), in0=b[a, t][:], in1=gain[a, t][:], op=MULT)
+
+        for t in range(3):
+            throws(0, t)
+            place(0, t)
+        wa_q = {(g, 0): quantise_weight(f"wa{g}0", wa_raw[g, 0]) for g in range(2)}
+
+        v_s = held("v_s", [P, S], U8)
+        v_w = [held(f"v_w{g}", [P, S], U32) for g in range(2)]
+        nc.vector.tensor_copy(out=v_s[:], in_=tab_s[:].indirect(offs_t[:]))
+        for g in range(2):
+            nc.vector.tensor_copy(out=v_w[g][:], in_=tab_w[g][:].bitcast(U32).indirect(offs_t[:]))
+
+        for t in (1, 2, 3):
+            throws(1, t)
+        for a, t in ((0, 3), (1, 0)):
+            throws(a, t)
+            place(a, t)
+        for g in range(2):
+            wa_q[g, 1] = quantise_weight(f"wa{g}1", wa_raw[g, 1])
+
+        z = [held(f"z{a}", [P, PACK, S], F32, tag=f"wide{a}") for a in range(2)]
+
+        def plane_tile(name, shape, dtype):
+            return ring.tile(shape, dtype, name=name, tag="planes", bufs=4, align_bytes=64)
+
+        def features(a, t):
+            act = plane_tile(f"act{a}{t}", [P, S], F32)
+            for j0 in range(0, S, BANK):
+                cols = slice(j0, j0 + BANK)
+                bank = bank_tile(f"pa{a}{t}{j0}", BANK)
+                product(bank[:], [wa_q[g, a] for g in range(2)], P * t, [(v_w[g][:, cols], v_s[4 * g :, cols]) for g in range(2)])
+                nc.scalar.activation(out=act[:, cols], in_=bank[:], func=ACT.Silu)
+            return act
+
+        def make_z(a, t, act, j0, width):
+            cols = slice(j0, j0 + width)
+            nc.vector.scalar_tensor_tensor(
+                out=z[a][:, t, cols], in0=act[:, cols], scalar=gz_t[:, a, t : t + 1], in1=page_of(a, t)[:, cols], op0=MULT, op1=ADD
+            )
+
+        def weave(engine, grouped, planes):
+            dst = grouped[:].rearrange("p (c i t) -> p c t i", i=4, t=PACK)
+            src = planes.rearrange("p t (c i) -> p c t i", i=4)
+            if engine == "scalar":
+                nc.scalar.copy(out=dst, in_=src)
+            else:
+                nc.vector.tensor_copy(out=dst, in_=src)
+
+        w2_q = {}
+        z_q = {}
+
+        def quantise_w2(g, h):
+            w2_q[g, h] = quantise_weight(f"w2{g}{h}", w2_raw[g, h])
+
+        def quantise_z(a, j0, engine):
+            grouped = grouped_tile(f"z_grouped{a}{j0}", BANK)
+            weave(engine, grouped, z[a][:, :, j0 : j0 + BANK])
+            z_q[a, j0] = quantise(f"z{a}{j0}", grouped, BANK)
+
+        for pair in range(2):
+            for t in (2 * pair, 2 * pair + 1):
+                make_z(0, t, features(0, t), 0, S)
+            place(1, pair + 1)
+            quantise_w2(*quarters[pair])
+        for t in range(2):
+            make_z(1, t, features(1, t), 0, S)
+        for gh in quarters[2:]:
+            quantise_w2(*gh)
+        quantise_z(0, 0, "scalar")
+        make_z(1, 2, features(1, 2), 0, S)
+        place(1, 3)
+        last = features(1, 3)
+        quantise_z(0, BANK, "scalar")
+        for j0 in range(0, S, BANK):
+            make_z(1, 3, last, j0, BANK)
+            quantise_z(1, j0, Z_WEAVE[j0 // BANK])
+
+        y = {}
+        y_q = {}
+
+        def make_y(ci, a):
+            j0, width = CHUNKS[ci]
+            half = j0 // BANK * BANK
+            part = slice(j0 - half, j0 - half + width)
+            moving = [(z_q[g, half][0][:, part], z_q[g, half][1][:, part]) for g in range(2)]
+            per_bank = BANK // width
+            y[ci, a] = plane_tile(f"y{a}{ci}", [P, PACK, width], BF16)
+            for t0 in range(0, PACK, per_bank):
+                bank = bank_tile(f"u{a}{t0}{ci}", BANK)
+                for u in range(per_bank):
+                    product(bank[:, width * u : width * (u + 1)], [w2_q[g, a] for g in range(2)], P * (t0 + u), moving)
+                th = row_tile(f"th{a}{t0}{ci}", BANK)
+                nc.scalar.activation(out=th[:], in_=bank[:], func=ACT.Tanh)
+                for u in range(per_bank):
+                    t = t0 + u
+                    nc.vector.scalar_tensor_tensor(
+                        out=y[ci, a][:, t, :], in0=th[:, width * u : width * (u + 1)], scalar=gt_t[:, a, t : t + 1],
+                        in1=z[a][:, t, j0 : j0 + width], op0=MULT, op1=ADD,
+                    )
+
+        def quantise_y(ci, a):
+            width = CHUNKS[ci][1]
+            grouped = grouped_tile(f"y_grouped{a}{ci}", width)
+            weave(Y_WEAVE[ci][a], grouped, y[ci, a][:])
+            codes, scales = quantise(f"y{a}{ci}", grouped, width)
+            y_q[ci, a] = (codes[:], scales[:])
+
+        def scores(ci):
+            j0, width = CHUNKS[ci]
+            for n0 in range(0, N, P):
+                bank = bank_tile(f"o{ci}{n0}", width)
+                product(bank[:], [(w3_w[:, g, :], w3_s[:, N * g : N * (g + 1)]) for g in range(2)], n0, [y_q[ci, a] for a in range(2)])
+                res = row_tile(f"res{ci}{n0}", width)
+                if ci == len(CHUNKS) - 1 and n0 == P:
+                    nc.vector.tensor_copy(out=res[:], in_=bank[:])
+                else:
+                    nc.scalar.copy(out=res[:], in_=bank[:])
+                nc.sync.dma_start(out[n0 : n0 + P, j0 : j0 + width], res[:])
+
+        steps = [(ci, a) for ci in range(len(CHUNKS)) for a in range(2)]
+        for i, step in enumerate(steps):
+            make_y(*step)
+            if i >= 1:
+                quantise_y(*steps[i - 1])
+            if i >= 3 and i % 2 == 1:
+                scores(step[0] - 1)
+        quantise_y(*steps[-1])
+        scores(len(CHUNKS) - 1)

@@ -22,8 +22,10 @@ KP = P * PACK
 T, TB, S, NP, H, N = 4096, 2048, 1024, 512, 1024, 384
 BANK = 512
 CHUNKS = ((0, 512), (512, 512))
-Y_WEAVE = (("vector","scalar"),("scalar","vector"))
-Z_WEAVE = ("vector","scalar")
+Y_WEAVE = (("vector", "scalar"), ("scalar", "vector"))
+RAW_SLOT = {("w2", 0, 0): "tab2_w", ("w2", 1, 0): "wa_raw00", ("w2", 0, 1): "wa_raw01", ("w2", 1, 1): "wgs_t"}
+EARLY = 3
+Z_WEAVE = ("vector", "scalar")
 
 
 def tile_list_pitch_delivery_scores_kernel(
@@ -39,14 +41,11 @@ def tile_list_pitch_delivery_scores_kernel(
         def held(name, shape, dtype, tag=None):
             return keep.tile(shape, dtype, name=name, tag=tag or name, align_bytes=64)
 
-        def raw_tile(name):
-            return ring.tile([P, PACK, KP], F32, name=name, tag="raw", bufs=4, align_bytes=64)
-
         def grouped_tile(name, cols):
-            return ring.tile([P, cols * PACK], BF16, name=name, tag="grouped", bufs=5, align_bytes=64)
+            return ring.tile([P, cols * PACK], BF16, name=name, tag="grouped", bufs=4, align_bytes=64)
 
         def row_tile(name, cols):
-            return ring.tile([P, cols], F32, name=name, tag="row", bufs=8, align_bytes=64)
+            return ring.tile([P, cols], F32, name=name, tag="row", bufs=6, align_bytes=64)
 
         def bank_tile(name, cols):
             return psum.tile([P, cols], F32, name=name, tag="bank")
@@ -70,42 +69,43 @@ def tile_list_pitch_delivery_scores_kernel(
         warm = held("warm", [P, 1], F32)
         placed = [held(f"placed{t}", [P, S], F32) for t in range(PACK + 1)]
 
-        nc.gpsimd.memset(tab2_s[:].bitcast(I32), 0)
+        nc.vector.memset(tab2_s[:].bitcast(I32), 0)
         nc.vector.memset(wb_s[:].bitcast(I32), 0)
         nc.vector.memset(one[:], 1.0)
         nc.vector.memset(tab_s[:].bitcast(I32), 0)
         nc.vector.memset(w3_s[:].bitcast(I32), 0)
         for page in placed:
             nc.vector.memset(page[:], 0.0)
-        nc.scalar.activation(out=warm[:], in_=one[:], func=ACT.Abs_reciprocal_sqrt, bias=one[:])
 
+        nc.scalar.dma_start(gz_t[:], gz.rearrange("(a p t) -> p a t", a=2, t=PACK))
+        nc.scalar.dma_start(gt_t[:], gt.rearrange("(a p t) -> p a t", a=2, t=PACK))
+        nc.scalar.dma_start(wb_w[:].bitcast(I32), wb_words[0].bitcast(I32))
+        nc.scalar.dma_start(tab2_w[:], tab2_words[0].rearrange("p t i -> p (t i)").bitcast(I32))
+        nc.scalar.activation(out=warm[:], in_=one[:], func=ACT.Abs_reciprocal_sqrt, bias=one[:])
         nc.sync.dma_start(offs2_t[:], offs2)
         nc.sync.dma_start(pos_t[:], pos1)
-        nc.sync.dma_start(gz_t[:], gz.rearrange("(a p t) -> p a t", a=2, t=PACK))
-        nc.sync.dma_start(offs_t[:], offs)
-        nc.sync.dma_start(gt_t[:], gt.rearrange("(a p t) -> p a t", a=2, t=PACK))
-        nc.sync.dma_start(wb_w[:].bitcast(I32), wb_words[0].bitcast(I32))
-        nc.sync.dma_start(tab2_w[:], tab2_words[0].rearrange("p t i -> p (t i)").bitcast(I32))
+        for q in range(4):
+            nc.sync.dma_start(tab2_s[32 * q : 32 * q + 4, :].bitcast(I32), tab2_scales[0, 4 * q : 4 * q + 4, :].bitcast(I32))
         for q in range(4):
             nc.sync.dma_start(wb_s[32 * q : 32 * q + 4, :].bitcast(I32), wb_scales[0, 4 * q : 4 * q + 4, :].bitcast(I32))
         for q in range(4):
-            queue = nc.sync if q < 2 else nc.gpsimd
-            queue.dma_start(tab2_s[32 * q : 32 * q + 4, :].bitcast(I32), tab2_scales[0, 4 * q : 4 * q + 4, :].bitcast(I32))
-        for q in range(4):
             nc.sync.dma_start(wgs_t[32 * q : 32 * q + 32, :], wgs.rearrange("(p t) j -> p (t j)", t=PACK))
+        nc.sync.dma_start(offs_t[:], offs)
 
         def load_weight(w, name, g, h):
-            raw = raw_tile(f"{name}_raw{g}{h}")
+            raw = held(f"{name}_raw{g}{h}", [P, PACK, KP], F32, tag=RAW_SLOT.get((name, g, h)))
             nc.sync.dma_start(raw[:], w[KP * g : KP * (g + 1), KP * h : KP * (h + 1)].rearrange("(p i) c -> p i c", i=PACK))
             return raw
 
+        wa_raw = {}
         for q in range(4):
             nc.sync.dma_start(tab_s[32 * q : 32 * q + 8, :].bitcast(I32), tab_scales[:, 4 * q : 4 * q + 4, :].bitcast(I32))
-        wa_raw = {(g, 0): load_weight(wa, "wa", g, 0) for g in range(2)}
-        for g in range(2):
-            nc.sync.dma_start(tab_w[g][:], tab_words[g].rearrange("p t i -> p (t i)").bitcast(I32))
-        for g in range(2):
-            wa_raw[g, 1] = load_weight(wa, "wa", g, 1)
+        wa_raw[0, 0] = load_weight(wa, "wa", 0, 0)
+        wa_raw[1, 0] = load_weight(wa, "wa", 1, 0)
+        nc.sync.dma_start(tab_w[0][:], tab_words[0].rearrange("p t i -> p (t i)").bitcast(I32))
+        nc.sync.dma_start(tab_w[1][:], tab_words[1].rearrange("p t i -> p (t i)").bitcast(I32))
+        wa_raw[0, 1] = load_weight(wa, "wa", 0, 1)
+        wa_raw[1, 1] = load_weight(wa, "wa", 1, 1)
         quarters = [(g, h) for h in range(2) for g in range(2)]
         w2_raw = {gh: load_weight(w2, "w2", *gh) for gh in quarters}
         for q in range(4):
@@ -156,15 +156,15 @@ def tile_list_pitch_delivery_scores_kernel(
                 out=wbd_s[:, cols].rearrange("p (t m) -> p t m", t=PACK), in_=wb_s[:, cols].rearrange("p (m t) -> p t m", t=PACK)
             )
 
-        deal_scales(0)
-        nc.vector.tensor_copy(out=v2_s[:], in_=tab2_s[:].indirect(offs2_t[:]))
         nc.vector.tensor_copy(out=v2_w[:], in_=tab2_w[:].bitcast(U32).indirect(offs2_t[:]))
+        nc.vector.tensor_copy(out=v2_s[:], in_=tab2_s[:].indirect(offs2_t[:]))
+        deal_scales(0)
         deal_scales(1)
 
         b = {}
         gain = {}
 
-        def throws(a, t):
+        def throws(a, t, dst):
             c0 = KP * a + P * t
             bank = bank_tile(f"q{a}{t}", NP)
             nc.tensor.matmul_mx(
@@ -176,7 +176,7 @@ def tile_list_pitch_delivery_scores_kernel(
                 start=True,
                 stop=True,
             )
-            b[a, t] = row_tile(f"b{a}{t}", NP)
+            b[a, t] = dst
             parts = [slice(0, NP // 2), slice(NP // 2, NP)] if (a, t) == (0, 0) else [slice(0, NP)]
             for cols in parts:
                 nc.scalar.activation(out=b[a, t][:, cols], in_=bank[:, cols], func=ACT.Square)
@@ -184,19 +184,23 @@ def tile_list_pitch_delivery_scores_kernel(
                 nc.scalar.activation(out=b[a, t][:, cols], in_=b[a, t][:, cols], func=ACT.Abs_reciprocal_sqrt, bias=one[:])
             for cols in parts:
                 nc.scalar.activation(out=b[a, t][:, cols], in_=b[a, t][:, cols], func=ACT.Square)
-            gain[a, t] = held(f"gain{a}{t}", [P, NP], F32)
+
+        def make_gain(a, t, dst):
+            gain[a, t] = dst
             nc.vector.tensor_scalar(
-                out=gain[a, t][:], in0=wgs_t[:, NP * t : NP * (t + 1)], scalar1=gz_t[:, a, t : t + 1], scalar2=None, op0=MULT
+                out=dst, in0=wgs_t[:, NP * t : NP * (t + 1)], scalar1=gz_t[:, a, t : t + 1], scalar2=None, op0=MULT
             )
 
         def page_of(a, t):
             return placed[t if a == 0 else (4, 1, 3, 3)[t]]
 
         def place(a, t):
-            nc.vector.tensor_tensor(out=page_of(a, t)[:].indirect(pos_t[:]), in0=b[a, t][:], in1=gain[a, t][:], op=MULT)
+            nc.vector.tensor_tensor(out=page_of(a, t)[:].indirect(pos_t[:]), in0=b[a, t], in1=gain[a, t], op=MULT)
 
-        for t in range(3):
-            throws(0, t)
+        early_gains = held("early_gains", [P, EARLY, NP], F32)
+        for t in range(EARLY):
+            throws(0, t, row_tile(f"b0{t}", NP)[:])
+            make_gain(0, t, early_gains[:, t, :])
             place(0, t)
         wa_q = {(g, 0): quantise_weight(f"wa{g}0", wa_raw[g, 0]) for g in range(2)}
 
@@ -206,21 +210,26 @@ def tile_list_pitch_delivery_scores_kernel(
         for g in range(2):
             nc.vector.tensor_copy(out=v_w[g][:], in_=tab_w[g][:].bitcast(U32).indirect(offs_t[:]))
 
-        for t in (1, 2, 3):
-            throws(1, t)
-        for a, t in ((0, 3), (1, 0)):
-            throws(a, t)
+        late = [(0, t) for t in range(EARLY, PACK)] + [(1, t) for t in range(PACK)]
+        late_gains = held("late_gains", [P, len(late), NP], F32, tag="wide1")
+        late_b = held("late_b_gains", [P, PACK, NP], F32, tag="wa_raw10")
+        for i, (a, t) in enumerate(late):
+            throws(a, t, late_b[:, t, :] if a == 1 else row_tile(f"b0{t}", NP)[:])
+            make_gain(a, t, late_gains[:, i, :])
+        for a, t in late[: PACK - EARLY + 1]:
             place(a, t)
         for g in range(2):
             wa_q[g, 1] = quantise_weight(f"wa{g}1", wa_raw[g, 1])
 
-        z = [held(f"z{a}", [P, PACK, S], F32, tag=f"wide{a}") for a in range(2)]
+        z = [held(f"z{a}", [P, PACK, S], F32, tag=("wide0", "z1")[a]) for a in range(2)]
 
         def plane_tile(name, shape, dtype):
             return ring.tile(shape, dtype, name=name, tag="planes", bufs=4, align_bytes=64)
 
+        first_acts = held("first_acts_gains", [P, 2, S], F32, tag="wa_raw11")
+
         def features(a, t):
-            act = plane_tile(f"act{a}{t}", [P, S], F32)
+            act = first_acts[:, t, :] if a == 0 and t < 2 else plane_tile(f"act{a}{t}", [P, S], F32)
             for j0 in range(0, S, BANK):
                 cols = slice(j0, j0 + BANK)
                 bank = bank_tile(f"pa{a}{t}{j0}", BANK)

@@ -23,7 +23,10 @@ T, TB, S, NP, H, N = 4096, 2048, 1024, 512, 1024, 384
 BANK = 512
 CHUNKS = ((0, 512), (512, 512))
 Y_WEAVE = (("vector", "scalar"), ("scalar", "vector"))
-RAW_SLOT = {("w2", 0, 0): "tab2_w", ("w2", 1, 0): "wa_raw00", ("w2", 0, 1): "wa_raw01", ("w2", 1, 1): "wgs_t"}
+RAW_SLOT = {("w2", 0, 0): "tab2_w", ("w2", 1, 0): "wa_raw00", ("w2", 1, 1): "wgs_t"}
+TAIL = 2
+PL = 3
+OUT_ENGINE = ("sss", "vsv", "vsv")
 EARLY = 3
 Z_WEAVE = ("vector", "scalar")
 
@@ -45,7 +48,7 @@ def tile_list_pitch_delivery_scores_kernel(
             return ring.tile([P, cols * PACK], BF16, name=name, tag="grouped", bufs=4, align_bytes=64)
 
         def row_tile(name, cols):
-            return ring.tile([P, cols], F32, name=name, tag="row", bufs=6, align_bytes=64)
+            return ring.tile([P, cols], F32, name=name, tag="row", bufs=5, align_bytes=64)
 
         def bank_tile(name, cols):
             return psum.tile([P, cols], F32, name=name, tag="bank")
@@ -83,23 +86,29 @@ def tile_list_pitch_delivery_scores_kernel(
         nc.scalar.dma_start(tab2_w[:], tab2_words[0].rearrange("p t i -> p (t i)").bitcast(I32))
         nc.scalar.activation(out=warm[:], in_=one[:], func=ACT.Abs_reciprocal_sqrt, bias=one[:])
         nc.sync.dma_start(offs2_t[:], offs2)
-        nc.sync.dma_start(pos_t[:], pos1)
+        nc.sync.dma_start(offs_t[:], offs)
         for q in range(4):
             nc.sync.dma_start(tab2_s[32 * q : 32 * q + 4, :].bitcast(I32), tab2_scales[0, 4 * q : 4 * q + 4, :].bitcast(I32))
         for q in range(4):
             nc.sync.dma_start(wb_s[32 * q : 32 * q + 4, :].bitcast(I32), wb_scales[0, 4 * q : 4 * q + 4, :].bitcast(I32))
         for q in range(4):
             nc.sync.dma_start(wgs_t[32 * q : 32 * q + 32, :], wgs.rearrange("(p t) j -> p (t j)", t=PACK))
-        nc.sync.dma_start(offs_t[:], offs)
+
+        wa_half1 = held("wa_half1", [P, 2, PACK, KP], F32)
 
         def load_weight(w, name, g, h):
-            raw = held(f"{name}_raw{g}{h}", [P, PACK, KP], F32, tag=RAW_SLOT.get((name, g, h)))
-            nc.sync.dma_start(raw[:], w[KP * g : KP * (g + 1), KP * h : KP * (h + 1)].rearrange("(p i) c -> p i c", i=PACK))
+            if (name, h) == ("wa", 1):
+                raw = wa_half1[:, g, :, :]
+            else:
+                raw = held(f"{name}_raw{g}{h}", [P, PACK, KP], F32, tag=RAW_SLOT.get((name, g, h)))[:]
+            nc.sync.dma_start(raw, w[KP * g : KP * (g + 1), KP * h : KP * (h + 1)].rearrange("(p i) c -> p i c", i=PACK))
             return raw
 
         wa_raw = {}
         for q in range(4):
             nc.sync.dma_start(tab_s[32 * q : 32 * q + 8, :].bitcast(I32), tab_scales[:, 4 * q : 4 * q + 4, :].bitcast(I32))
+            if q == 0:
+                nc.sync.dma_start(pos_t[:], pos1)
         wa_raw[0, 0] = load_weight(wa, "wa", 0, 0)
         wa_raw[1, 0] = load_weight(wa, "wa", 1, 0)
         nc.sync.dma_start(tab_w[0][:], tab_words[0].rearrange("p t i -> p (t i)").bitcast(I32))
@@ -125,7 +134,7 @@ def tile_list_pitch_delivery_scores_kernel(
             grouped = grouped_tile(f"{name}_grouped", KP)
             nc.scalar.copy(
                 out=grouped[:].rearrange("p (t m i) -> p m i t", t=PACK, i=PACK),
-                in_=raw[:].rearrange("p i (m t) -> p m i t", t=PACK),
+                in_=raw.rearrange("p i (m t) -> p m i t", t=PACK),
             )
             return quantise(name, grouped, KP)
 
@@ -224,12 +233,12 @@ def tile_list_pitch_delivery_scores_kernel(
         z = [held(f"z{a}", [P, PACK, S], F32, tag=("wide0", "z1")[a]) for a in range(2)]
 
         def plane_tile(name, shape, dtype):
-            return ring.tile(shape, dtype, name=name, tag="planes", bufs=4, align_bytes=64)
+            return ring.tile(shape, dtype, name=name, tag="planes", bufs=PL, align_bytes=64)
 
-        first_acts = held("first_acts_gains", [P, 2, S], F32, tag="wa_raw11")
+        first_acts = held("first_acts_gains", [P, PACK, S], F32, tag="wa_half1")
 
         def features(a, t):
-            act = first_acts[:, t, :] if a == 0 and t < 2 else plane_tile(f"act{a}{t}", [P, S], F32)
+            act = first_acts[:, t, :] if a == 0 else plane_tile(f"act{a}{t}", [P, S], F32)
             for j0 in range(0, S, BANK):
                 cols = slice(j0, j0 + BANK)
                 bank = bank_tile(f"pa{a}{t}{j0}", BANK)
@@ -304,23 +313,29 @@ def tile_list_pitch_delivery_scores_kernel(
                     )
 
         def quantise_y(ci, a):
-            width = CHUNKS[ci][1]
-            grouped = grouped_tile(f"y_grouped{a}{ci}", width)
-            weave(Y_WEAVE[ci][a], grouped, y[ci, a][:])
-            codes, scales = quantise(f"y{a}{ci}", grouped, width)
-            y_q[ci, a] = (codes[:], scales[:])
+            parts = TAIL if ci == len(CHUNKS) - 1 else 1
+            width = CHUNKS[ci][1] // parts
+            for h in range(parts):
+                grouped = grouped_tile(f"y_grouped{a}{ci}{h}", width)
+                weave(Y_WEAVE[ci][a], grouped, y[ci, a][:, :, width * h : width * (h + 1)])
+                codes, scales = quantise(f"y{a}{ci}{h}", grouped, width)
+                y_q[ci, a, h] = (codes[:], scales[:])
 
-        def scores(ci):
+        def scores(ci, h=0):
             j0, width = CHUNKS[ci]
+            if ci == len(CHUNKS) - 1:
+                width = width // TAIL
+                j0 = j0 + width * h
+            staged = held(f"res{ci}{h}_gains", [P, N // P, width], F32, tag=("tab2_w", "wa_raw00", "wgs_t")[ci + h])
             for n0 in range(0, N, P):
-                bank = bank_tile(f"o{ci}{n0}", width)
-                product(bank[:], [(w3_w[:, g, :], w3_s[:, N * g : N * (g + 1)]) for g in range(2)], n0, [y_q[ci, a] for a in range(2)])
-                res = row_tile(f"res{ci}{n0}", width)
-                if ci == len(CHUNKS) - 1 and n0 == P:
-                    nc.vector.tensor_copy(out=res[:], in_=bank[:])
+                bank = bank_tile(f"o{ci}{n0}{h}", width)
+                product(bank[:], [(w3_w[:, g, :], w3_s[:, N * g : N * (g + 1)]) for g in range(2)], n0, [y_q[ci, a, h] for a in range(2)])
+                res = staged[:, n0 // P, :]
+                if OUT_ENGINE[ci + h][n0 // P] == "v":
+                    nc.vector.tensor_copy(out=res, in_=bank[:])
                 else:
-                    nc.scalar.copy(out=res[:], in_=bank[:])
-                nc.sync.dma_start(out[n0 : n0 + P, j0 : j0 + width], res[:])
+                    nc.scalar.copy(out=res, in_=bank[:])
+                nc.sync.dma_start(out[n0 : n0 + P, j0 : j0 + width], res)
 
         steps = [(ci, a) for ci in range(len(CHUNKS)) for a in range(2)]
         for i, step in enumerate(steps):
@@ -330,4 +345,5 @@ def tile_list_pitch_delivery_scores_kernel(
             if i >= 3 and i % 2 == 1:
                 scores(step[0] - 1)
         quantise_y(*steps[-1])
-        scores(len(CHUNKS) - 1)
+        for h in range(TAIL):
+            scores(len(CHUNKS) - 1, h)

from contextlib import ExitStack

import concourse.mybir as mybir

F32 = mybir.dt.float32
BF16 = mybir.dt.bfloat16
I32 = mybir.dt.int32
U32 = mybir.dt.uint32
U16 = mybir.dt.uint16
U8 = mybir.dt.uint8
FP8X4 = mybir.dt.float8_e4m3fn_x4
FP4X4 = mybir.dt.float4_e2m1fn_x4
ACT = mybir.ActivationFunctionType
MULT = mybir.AluOpType.mult
ADD = mybir.AluOpType.add

FLOPS = 5637144576

P = 128
PACK = 4
KP = P * PACK
T, TB, S, NP, H, N = 4096, 2048, 1024, 512, 1024, 384
BANK = 512
CHUNKS = ((0, 512), (512, 512))
Y_WEAVE = (("vector", "scalar"), ("scalar", "vector"))
RAW_SLOT = {("w2", 0, 0): "tab2_w", ("w2", 1, 0): "wa_raw00", ("w2", 1, 1): "wgs_t"}
TAIL = 2
PL = 3
OUT_ENGINE = ("sss", "vsv", "vsv")
EARLY = 3
Z_WEAVE = ("vector", "scalar")


def tile_list_pitch_delivery_scores_kernel(
    tc, tab_words, tab_scales, offs, tab2_words, tab2_scales, offs2, pos1, wa, wb_words, wb_scales,
    wgs, gz, w2, gt, w3_words, w3_scales, out,
):
    nc = tc.nc
    with ExitStack() as ctx:
        keep = ctx.enter_context(tc.tile_pool(name="keep", bufs=1))
        ring = ctx.enter_context(tc.tile_pool(name="ring", bufs=1))
        psum = ctx.enter_context(tc.psum_pool(name="psum", bufs=8))

        def held(name, shape, dtype, tag=None):
            return keep.tile(shape, dtype, name=name, tag=tag or name, align_bytes=64)

        def grouped_tile(name, cols):
            return ring.tile([P, cols * PACK], BF16, name=name, tag="grouped", bufs=4, align_bytes=64)

        def row_tile(name, cols):
            return ring.tile([P, cols], F32, name=name, tag="row", bufs=5, align_bytes=64)

        def bank_tile(name, cols):
            return psum.tile([P, cols], F32, name=name, tag="bank")

        offs_t = held("offs_t", [P, S // 16], U16)
        offs2_t = held("offs2_t", [P, NP // 16], U16)
        pos_t = held("pos_t", [P, NP // 16], U16)

        tab2_w = held("tab2_w", [P, TB], I32)
        tab2_s = held("tab2_s", [P, TB], U8)
        wb_w = held("wb_w", [P, 2 * H], U8)
        wb_s = held("wb_s", [P, H], U8)
        tab_w = [held(f"tab_w{g}", [P, T], I32, tag=f"wide{g}") for g in range(2)]
        tab_s = held("tab_s", [P, T], U8)
        w3_w = held("w3_w", [P, 2, N], I32)
        w3_s = held("w3_s", [P, 2 * N], U8)
        wgs_t = held("wgs_t", [P, PACK * NP], F32)
        gz_t = held("gz_t", [P, 2, PACK], F32)
        gt_t = held("gt_t", [P, 2, PACK], F32)
        one = held("one", [P, 1], F32)
        warm = held("warm", [P, 1], F32)
        placed = [held(f"placed{t}", [P, S], F32) for t in range(PACK + 1)]

        nc.vector.memset(tab2_s[:].bitcast(I32), 0)
        nc.vector.memset(wb_s[:].bitcast(I32), 0)
        nc.vector.memset(one[:], 1.0)
        nc.vector.memset(tab_s[:].bitcast(I32), 0)
        nc.vector.memset(w3_s[:].bitcast(I32), 0)
        for page in placed:
            nc.vector.memset(page[:], 0.0)

        nc.scalar.dma_start(gz_t[:], gz.rearrange("(a p t) -> p a t", a=2, t=PACK))
        nc.scalar.dma_start(gt_t[:], gt.rearrange("(a p t) -> p a t", a=2, t=PACK))
        nc.scalar.dma_start(wb_w[:].bitcast(I32), wb_words[0].bitcast(I32))
        nc.scalar.dma_start(tab2_w[:], tab2_words[0].rearrange("p t i -> p (t i)").bitcast(I32))
        nc.scalar.activation(out=warm[:], in_=one[:], func=ACT.Abs_reciprocal_sqrt, bias=one[:])
        nc.sync.dma_start(offs2_t[:], offs2)
        nc.sync.dma_start(offs_t[:], offs)
        for q in range(4):
            nc.sync.dma_start(tab2_s[32 * q : 32 * q + 4, :].bitcast(I32), tab2_scales[0, 4 * q : 4 * q + 4, :].bitcast(I32))
        for q in range(4):
            nc.sync.dma_start(wb_s[32 * q : 32 * q + 4, :].bitcast(I32), wb_scales[0, 4 * q : 4 * q + 4, :].bitcast(I32))
        for q in range(4):
            nc.sync.dma_start(wgs_t[32 * q : 32 * q + 32, :], wgs.rearrange("(p t) j -> p (t j)", t=PACK))

        wa_half1 = held("wa_half1", [P, 2, PACK, KP], F32)

        def load_weight(w, name, g, h):
            if (name, h) == ("wa", 1):
                raw = wa_half1[:, g, :, :]
            else:
                raw = held(f"{name}_raw{g}{h}", [P, PACK, KP], F32, tag=RAW_SLOT.get((name, g, h)))[:]
            nc.sync.dma_start(raw, w[KP * g : KP * (g + 1), KP * h : KP * (h + 1)].rearrange("(p i) c -> p i c", i=PACK))
            return raw

        wa_raw = {}
        for q in range(4):
            nc.sync.dma_start(tab_s[32 * q : 32 * q + 8, :].bitcast(I32), tab_scales[:, 4 * q : 4 * q + 4, :].bitcast(I32))
            if q == 0:
                nc.sync.dma_start(pos_t[:], pos1)
        wa_raw[0, 0] = load_weight(wa, "wa", 0, 0)
        wa_raw[1, 0] = load_weight(wa, "wa", 1, 0)
        nc.sync.dma_start(tab_w[0][:], tab_words[0].rearrange("p t i -> p (t i)").bitcast(I32))
        nc.sync.dma_start(tab_w[1][:], tab_words[1].rearrange("p t i -> p (t i)").bitcast(I32))
        wa_raw[0, 1] = load_weight(wa, "wa", 0, 1)
        wa_raw[1, 1] = load_weight(wa, "wa", 1, 1)
        quarters = [(g, h) for h in range(2) for g in range(2)]
        w2_raw = {gh: load_weight(w2, "w2", *gh) for gh in quarters}
        for q in range(4):
            nc.sync.dma_start(
                w3_s[32 * q : 32 * q + 4, :].bitcast(I32).rearrange("r (g n) -> r g n", g=2),
                w3_scales[:, 4 * q : 4 * q + 4, :].bitcast(I32).rearrange("g r n -> r g n"),
            )
        nc.sync.dma_start(w3_w[:], w3_words.rearrange("g p n i -> p g (n i)").bitcast(I32))

        def quantise(name, grouped, cols):
            codes = held(f"{name}_c", [P, cols], U32)
            scales = held(f"{name}_s", [P, cols], U8)
            nc.vector.quantize_mx(out=codes[:].bitcast(FP8X4), scales=scales[:], in_=grouped[:])
            return codes, scales

        def quantise_weight(name, raw):
            grouped = grouped_tile(f"{name}_grouped", KP)
            nc.scalar.copy(
                out=grouped[:].rearrange("p (t m i) -> p m i t", t=PACK, i=PACK),
                in_=raw.rearrange("p i (m t) -> p m i t", t=PACK),
            )
            return quantise(name, grouped, KP)

        def product(acc, stationary, col0, moving):
            cols = slice(col0, col0 + P)
            for g in range(2):
                nc.tensor.matmul_mx(
                    out=acc,
                    lhsT=stationary[g][0][:, cols].bitcast(FP8X4),
                    lhsT_scale=stationary[g][1][:, cols],
                    rhs=moving[g][0].bitcast(FP8X4),
                    rhs_scale=moving[g][1],
                    start=(g == 0),
                    stop=(g == 1),
                )

        wbd_w = held("wbd_w", [P, 2 * H], U8)
        wbd_s = held("wbd_s", [P, H], U8)
        v2_w = held("v2_w", [P, NP], U32)
        v2_s = held("v2_s", [P, NP], U8)
        nc.vector.tensor_copy(
            out=wbd_w[:].bitcast(U16).rearrange("p (a t m) -> p a t m", a=2, t=PACK),
            in_=wb_w[:].bitcast(U16).rearrange("p (a m t) -> p a t m", a=2, t=PACK),
        )
        def deal_scales(a):
            cols = slice(KP * a, KP * (a + 1))
            nc.vector.tensor_copy(
                out=wbd_s[:, cols].rearrange("p (t m) -> p t m", t=PACK), in_=wb_s[:, cols].rearrange("p (m t) -> p t m", t=PACK)
            )

        nc.vector.tensor_copy(out=v2_w[:], in_=tab2_w[:].bitcast(U32).indirect(offs2_t[:]))
        nc.vector.tensor_copy(out=v2_s[:], in_=tab2_s[:].indirect(offs2_t[:]))
        deal_scales(0)
        deal_scales(1)

        b = {}
        gain = {}

        def throws(a, t, dst):
            c0 = KP * a + P * t
            bank = bank_tile(f"q{a}{t}", NP)
            nc.tensor.matmul_mx(
                out=bank[:],
                lhsT=wbd_w[:, 2 * c0 : 2 * (c0 + P)].bitcast(FP4X4),
                lhsT_scale=wbd_s[:, c0 : c0 + P],
                rhs=v2_w[:].bitcast(FP8X4),
                rhs_scale=v2_s[:],
                start=True,
                stop=True,
            )
            b[a, t] = dst
            parts = [slice(0, NP // 2), slice(NP // 2, NP)] if (a, t) == (0, 0) else [slice(0, NP)]
            for cols in parts:
                nc.scalar.activation(out=b[a, t][:, cols], in_=bank[:, cols], func=ACT.Square)
            for cols in parts:
                nc.scalar.activation(out=b[a, t][:, cols], in_=b[a, t][:, cols], func=ACT.Abs_reciprocal_sqrt, bias=one[:])
            for cols in parts:
                nc.scalar.activation(out=b[a, t][:, cols], in_=b[a, t][:, cols], func=ACT.Square)

        def make_gain(a, t, dst):
            gain[a, t] = dst
            nc.vector.tensor_scalar(
                out=dst, in0=wgs_t[:, NP * t : NP * (t + 1)], scalar1=gz_t[:, a, t : t + 1], scalar2=None, op0=MULT
            )

        def page_of(a, t):
            return placed[t if a == 0 else (4, 1, 3, 3)[t]]

        def place(a, t):
            nc.vector.tensor_tensor(out=page_of(a, t)[:].indirect(pos_t[:]), in0=b[a, t], in1=gain[a, t], op=MULT)

        early_gains = held("early_gains", [P, EARLY, NP], F32)
        for t in range(EARLY):
            throws(0, t, row_tile(f"b0{t}", NP)[:])
            make_gain(0, t, early_gains[:, t, :])
            place(0, t)
        wa_q = {(g, 0): quantise_weight(f"wa{g}0", wa_raw[g, 0]) for g in range(2)}

        v_s = held("v_s", [P, S], U8)
        v_w = [held(f"v_w{g}", [P, S], U32) for g in range(2)]
        nc.vector.tensor_copy(out=v_s[:], in_=tab_s[:].indirect(offs_t[:]))
        for g in range(2):
            nc.vector.tensor_copy(out=v_w[g][:], in_=tab_w[g][:].bitcast(U32).indirect(offs_t[:]))

        late = [(0, t) for t in range(EARLY, PACK)] + [(1, t) for t in range(PACK)]
        late_gains = held("late_gains", [P, len(late), NP], F32, tag="wide1")
        late_b = held("late_b_gains", [P, PACK, NP], F32, tag="wa_raw10")
        for i, (a, t) in enumerate(late):
            throws(a, t, late_b[:, t, :] if a == 1 else row_tile(f"b0{t}", NP)[:])
            make_gain(a, t, late_gains[:, i, :])
        for a, t in late[: PACK - EARLY + 1]:
            place(a, t)
        for g in range(2):
            wa_q[g, 1] = quantise_weight(f"wa{g}1", wa_raw[g, 1])

        z = [held(f"z{a}", [P, PACK, S], F32, tag=("wide0", "z1")[a]) for a in range(2)]

        def plane_tile(name, shape, dtype):
            return ring.tile(shape, dtype, name=name, tag="planes", bufs=PL, align_bytes=64)

        first_acts = held("first_acts_gains", [P, PACK, S], F32, tag="wa_half1")

        def features(a, t):
            act = first_acts[:, t, :] if a == 0 else plane_tile(f"act{a}{t}", [P, S], F32)
            for j0 in range(0, S, BANK):
                cols = slice(j0, j0 + BANK)
                bank = bank_tile(f"pa{a}{t}{j0}", BANK)
                product(bank[:], [wa_q[g, a] for g in range(2)], P * t, [(v_w[g][:, cols], v_s[4 * g :, cols]) for g in range(2)])
                nc.scalar.activation(out=act[:, cols], in_=bank[:], func=ACT.Silu)
            return act

        def make_z(a, t, act, j0, width):
            cols = slice(j0, j0 + width)
            nc.vector.scalar_tensor_tensor(
                out=z[a][:, t, cols], in0=act[:, cols], scalar=gz_t[:, a, t : t + 1], in1=page_of(a, t)[:, cols], op0=MULT, op1=ADD
            )

        def weave(engine, grouped, planes):
            dst = grouped[:].rearrange("p (c i t) -> p c t i", i=4, t=PACK)
            src = planes.rearrange("p t (c i) -> p c t i", i=4)
            if engine == "scalar":
                nc.scalar.copy(out=dst, in_=src)
            else:
                nc.vector.tensor_copy(out=dst, in_=src)

        w2_q = {}
        z_q = {}

        def quantise_w2(g, h):
            w2_q[g, h] = quantise_weight(f"w2{g}{h}", w2_raw[g, h])

        def quantise_z(a, j0, engine):
            grouped = grouped_tile(f"z_grouped{a}{j0}", BANK)
            weave(engine, grouped, z[a][:, :, j0 : j0 + BANK])
            z_q[a, j0] = quantise(f"z{a}{j0}", grouped, BANK)

        for pair in range(2):
            for t in (2 * pair, 2 * pair + 1):
                make_z(0, t, features(0, t), 0, S)
            place(1, pair + 1)
            quantise_w2(*quarters[pair])
        for t in range(2):
            make_z(1, t, features(1, t), 0, S)
        for gh in quarters[2:]:
            quantise_w2(*gh)
        quantise_z(0, 0, "scalar")
        make_z(1, 2, features(1, 2), 0, S)
        place(1, 3)
        last = features(1, 3)
        quantise_z(0, BANK, "scalar")
        for j0 in range(0, S, BANK):
            make_z(1, 3, last, j0, BANK)
            quantise_z(1, j0, Z_WEAVE[j0 // BANK])

        y = {}
        y_q = {}

        def make_y(ci, a):
            j0, width = CHUNKS[ci]
            half = j0 // BANK * BANK
            part = slice(j0 - half, j0 - half + width)
            moving = [(z_q[g, half][0][:, part], z_q[g, half][1][:, part]) for g in range(2)]
            per_bank = BANK // width
            y[ci, a] = plane_tile(f"y{a}{ci}", [P, PACK, width], BF16)
            for t0 in range(0, PACK, per_bank):
                bank = bank_tile(f"u{a}{t0}{ci}", BANK)
                for u in range(per_bank):
                    product(bank[:, width * u : width * (u + 1)], [w2_q[g, a] for g in range(2)], P * (t0 + u), moving)
                th = row_tile(f"th{a}{t0}{ci}", BANK)
                nc.scalar.activation(out=th[:], in_=bank[:], func=ACT.Tanh)
                for u in range(per_bank):
                    t = t0 + u
                    nc.vector.scalar_tensor_tensor(
                        out=y[ci, a][:, t, :], in0=th[:, width * u : width * (u + 1)], scalar=gt_t[:, a, t : t + 1],
                        in1=z[a][:, t, j0 : j0 + width], op0=MULT, op1=ADD,
                    )

        def quantise_y(ci, a):
            parts = TAIL if ci == len(CHUNKS) - 1 else 1
            width = CHUNKS[ci][1] // parts
            for h in range(parts):
                grouped = grouped_tile(f"y_grouped{a}{ci}{h}", width)
                weave(Y_WEAVE[ci][a], grouped, y[ci, a][:, :, width * h : width * (h + 1)])
                codes, scales = quantise(f"y{a}{ci}{h}", grouped, width)
                y_q[ci, a, h] = (codes[:], scales[:])

        def scores(ci, h=0):
            j0, width = CHUNKS[ci]
            if ci == len(CHUNKS) - 1:
                width = width // TAIL
                j0 = j0 + width * h
            staged = held(f"res{ci}{h}_gains", [P, N // P, width], F32, tag=("tab2_w", "wa_raw00", "wgs_t")[ci + h])
            for n0 in range(0, N, P):
                bank = bank_tile(f"o{ci}{n0}{h}", width)
                product(bank[:], [(w3_w[:, g, :], w3_s[:, N * g : N * (g + 1)]) for g in range(2)], n0, [y_q[ci, a, h] for a in range(2)])
                res = staged[:, n0 // P, :]
                if OUT_ENGINE[ci + h][n0 // P] == "v":
                    nc.vector.tensor_copy(out=res, in_=bank[:])
                else:
                    nc.scalar.copy(out=res, in_=bank[:])
                nc.sync.dma_start(out[n0 : n0 + P, j0 : j0 + width], res)

        steps = [(ci, a) for ci in range(len(CHUNKS)) for a in range(2)]
        for i, step in enumerate(steps):
            make_y(*step)
            if i >= 1:
                quantise_y(*steps[i - 1])
            if i >= 3 and i % 2 == 1:
                scores(step[0] - 1)
        quantise_y(*steps[-1])
        for h in range(TAIL):
            scores(len(CHUNKS) - 1, h)
